import numpy as np
import ml_dtypes


def mxq(x, axis, fmt="e4m3"):
    dtype, down = {"e4m3": (ml_dtypes.float8_e4m3fn, 7), "e5m2": (ml_dtypes.float8_e5m2, 14)}[fmt]
    v = np.moveaxis(np.asarray(x, np.float32).astype(ml_dtypes.bfloat16).astype(np.float64), axis, -1)
    blocks = v.reshape(v.shape[:-1] + (-1, 32))
    amax = np.abs(blocks).max(-1, keepdims=True)
    byte = np.maximum(np.where(amax > 0, np.frexp(amax)[1] - 1 + 127, 0) - down, 1)
    scale = np.exp2(byte - 127.0)
    codes = (blocks / scale).astype(np.float32).astype(dtype).astype(np.float64)
    return np.moveaxis((codes * scale).reshape(v.shape), -1, axis)


WIDE = False


def mx_kscale(k):
    if not WIDE:
        return np.ones(k)
    levels = np.array([10, -10, 5, -5, 0])
    if k % 512:
        return np.exp2(np.random.permutation(np.resize(levels, k // 32))).repeat(32)
    a = np.empty((k // 512, 16))
    for p in range(k // 512):
        a[p, :8] = np.random.permutation(np.resize(levels, 8))
        for g in range(8):
            far = levels[np.abs(levels - a[p, g]) >= 10]
            a[p, g + 8] = far[np.random.randint(len(far))]
    return np.exp2(a.ravel()).repeat(32)


def f64(x):
    return np.asarray(x).astype(np.float64)


def striped(idx):
    return np.tile(idx.reshape(-1, 16).T, (8, 1)).astype(np.uint16)


def unstriped(offs):
    return offs[:16].T.reshape(-1).astype(np.int64)


def striped8(idx):
    return np.concatenate([x.reshape(-1, 16).T for x in idx]).astype(np.uint16)


def runs(offs, k):
    lists = np.stack([offs[16 * r : 16 * r + 16].T.reshape(-1) for r in range(8)]).astype(np.int64)
    return lists[np.arange(k) % 512 // 64]


def pack_weight(w):
    k, n = w.shape
    w = f64(np.asarray(w, np.float32).astype(ml_dtypes.bfloat16)).reshape(k // 32, 32, n)
    amax = np.abs(w).max(1)
    byte = np.clip(np.where(amax > 0, np.frexp(amax)[1] - 1 + 127 - 7, 1), 1, 254)
    scaled = (w * np.exp2(127.0 - byte)[:, None, :]).reshape(k, n).astype(np.float32)
    words = np.ascontiguousarray(scaled.reshape(k // 512, 128, 4, n).transpose(0, 1, 3, 2)).astype(ml_dtypes.float8_e4m3fn).view(np.uint8)
    return words, np.ascontiguousarray(byte.astype(np.uint8).reshape(k // 512, 16, n))


def unpack_weight(words, scales):
    g, p, n, _ = words.shape
    vals = np.ascontiguousarray(words).view(ml_dtypes.float8_e4m3fn).astype(np.float64) * np.repeat(np.exp2(scales.astype(np.float64) - 127.0), 8, axis=1)[..., None]
    return vals.transpose(0, 1, 3, 2).reshape(g * 512, n)


def sigmoid(v):
    return 1.0 / (1.0 + np.exp(-np.maximum(v, -700.0)))

def planes(y):
    n, m = y.shape
    v = y.astype(np.float32).astype(ml_dtypes.bfloat16).astype(np.float64).reshape(n // 32, 32, m)
    top = np.abs(v).max(1)
    byte = np.clip(np.where(top > 0, np.frexp(top)[1] - 1 + 127 - 7, 1), 1, 254)
    codes = (v * np.exp2(127.0 - byte)[:, None, :]).reshape(n, m).astype(np.float32).astype(ml_dtypes.float8_e4m3fn).view(np.uint8)
    words = codes.reshape(n // 512, 128, 4, m).transpose(0, 1, 3, 2)
    return np.ascontiguousarray(words), np.ascontiguousarray(byte.astype(np.uint8).reshape(n // 512, 16, m))


K, T, S, H, J = 512, 2048, 512, 512, 512


def setup_inputs():
    n = np.random.standard_normal
    s = mx_kscale(K)[:, None]
    u = mx_kscale(H)
    packed_xT = pack_weight(n((K, T)) * s)
    packed_w1 = pack_weight(n((K, H)) / np.sqrt(K) / s)
    packed_w2 = pack_weight(n((H, H)) / np.sqrt(H) / u[:, None])
    return {
        "x_words": packed_xT[0],
        "x_scales": packed_xT[1],
        "w1_words": packed_w1[0],
        "w1_scales": packed_w1[1],
        "tab": n((H, J)).astype(np.float32),
        "gn": (np.random.uniform(0.5, 1.5, (H, 1)) * u[:, None]).astype(np.float32),
        "w2_words": packed_w2[0],
        "w2_scales": packed_w2[1],
        "offs": striped(np.random.permutation(T)[:S]),
        "n1": striped8(np.random.randint(0, J, (8, S))),
        "n2": striped8(np.stack([np.random.permutation(S) for _ in range(8)])),
        "n3": striped8(np.stack([np.random.permutation(S) for _ in range(8)])),
        "n4": striped8(np.stack([np.random.permutation(S) for _ in range(8)])),
        "n5": striped8(np.stack([np.random.permutation(S) for _ in range(8)])),
        "n6": striped8(np.stack([np.random.permutation(S) for _ in range(8)])),
    }


def reference(x_words, x_scales, w1_words, w1_scales, tab, gn, w2_words, w2_scales, offs, n1, n2, n3, n4, n5, n6):
    xq = unpack_weight(x_words, x_scales)[:, unstriped(offs)]
    y = unpack_weight(w1_words, w1_scales).T @ xq
    z = f64(gn) * (np.maximum(y + f64(tab)[np.arange(H)[:, None], runs(n1, H)], y[np.arange(H)[:, None], runs(n2, H)]))
    w2q = unpack_weight(w2_words, w2_scales)
    a = w2q.T @ mxq(z, 0, "e4m3")
    st = y * (sigmoid(y[np.arange(H)[:, None], runs(n3, H)]))
    z2 = f64(gn) * (st - (st[np.arange(H)[:, None], runs(n4, H)]))
    b = w2q.T @ mxq(z2, 0, "e4m3")
    out_0 = (a + a[np.arange(H)[:, None], runs(n5, H)]) * (sigmoid(b + b[np.arange(H)[:, None], runs(n6, H)]))
    return (out_0,) + planes(out_0)

@@ -1,0 +1,191 @@
+from contextlib import ExitStack
+
+import concourse.mybir as mybir
+
+F32 = mybir.dt.float32
+BF16 = mybir.dt.bfloat16
+I32 = mybir.dt.int32
+U32 = mybir.dt.uint32
+U16 = mybir.dt.uint16
+U8 = mybir.dt.uint8
+FP8X4 = mybir.dt.float8_e4m3fn_x4
+ALU = mybir.AluOpType
+ACT = mybir.ActivationFunctionType
+
+P = 128
+PACK = 4
+T = 2048
+S = 512
+H = 512
+FLOPS = 3 * 2 * 512 * 512 * 512
+
+
+def tile_picked_tietriebkindhopg_none_po_kernel(
+    tc, x_words, x_scales, w1_words, w1_scales, tab, gn, w2_words, w2_scales, offs, n1, n2, n3, n4, n5, n6, out_0, out_1, out_2
+):
+    nc = tc.nc
+    tiles = range(PACK)
+    with ExitStack() as ctx:
+        keep = ctx.enter_context(tc.tile_pool(name="keep", bufs=1))
+        psum = ctx.enter_context(tc.psum_pool(name="psum", bufs=1))
+
+        def sb(name, shape, dtype):
+            return keep.tile(shape, dtype, name=name, align_bytes=64)
+
+        def load_list(name, src):
+            tile = keep.tile([P, S // 16], U16, name=name)
+            nc.sync.dma_start(tile[:], src)
+            return tile
+
+        def load_words(name, src, width):
+            tile = sb(name, [P, width], U32)
+            nc.sync.dma_start(out=tile[:].bitcast(I32), in_=src[0].rearrange("p n t -> p (n t)").bitcast(I32))
+            return tile
+
+        def load_scales(name, src, width):
+            tile = sb(name, [P, width], U8)
+            nc.vector.memset(tile[:].bitcast(I32), 0)
+            for q in range(4):
+                nc.sync.dma_start(out=tile[32 * q : 32 * q + 4, :].bitcast(I32), in_=src[0, 4 * q : 4 * q + 4, :].bitcast(I32))
+            return tile
+
+        def load_scales_spread(tile, src, width, qs):
+            for q in qs:
+                rows = src[0, 4 * q : 4 * q + 4, :].bitcast(I32).unsqueeze(0).broadcast_to([8, 4, width // 4])
+                nc.sync.dma_start(out=tile[32 * q : 32 * q + 32, :].bitcast(I32), in_=rows)
+
+        def deal(name, tile, dtype, run):
+            dealt = sb(name, [P, H], dtype)
+            nc.vector.tensor_copy(
+                out=dealt[:].rearrange("p (t c i) -> p c t i", t=PACK, i=run),
+                in_=tile[:].rearrange("p (c i t) -> p c t i", t=PACK, i=run),
+            )
+            return dealt
+
+        def product(name, words, scales, parts, t):
+            acc = psum.tile([P, S], F32, name=name, tag="bank%d" % (t + (4 if name[0] == "a" else 0)))
+            cols = slice(P * t, P * (t + 1))
+            for rhs_words, rhs_scales, span in parts:
+                nc.tensor.matmul_mx(
+                    out=acc[:, span], lhsT=words[:, cols].bitcast(FP8X4), lhsT_scale=scales[:, cols],
+                    rhs=rhs_words[:].bitcast(FP8X4), rhs_scale=rhs_scales[:], start=True, stop=True,
+                )
+            return acc
+
+        def weave(engine_copy, woven, planes):
+            engine_copy(
+                out=woven.rearrange("p (c i) t -> p c t i", i=4),
+                in_=planes.rearrange("p t (c i) -> p c t i", i=4),
+            )
+
+        def quantise(name, woven, width):
+            words = sb(name + "_words", [P, width], U32)
+            scales = sb(name + "_scales", [P, width], U8)
+            nc.vector.quantize_mx(out=words[:].bitcast(FP8X4), scales=scales[:], in_=woven[:].rearrange("p n t -> p (n t)"))
+            return words, scales
+
+        def windows(name):
+            return [sb("%s%d" % (name, t), [P, 2 * S], F32) for t in tiles]
+
+        lo, hi = slice(0, S), slice(S, 2 * S)
+        whole = slice(0, S)
+
+        l_offs = load_list("l_offs", offs)
+        xs = sb("xs", [P, T], U8)
+        load_scales_spread(xs, x_scales, T, range(4))
+        xw = load_words("xw", x_words, T)
+        w1s = sb("w1s", [P, H], U8)
+        load_scales_spread(w1s, w1_scales, H, range(4))
+        w1w = load_words("w1w", w1_words, H)
+        tab_w, y_w, st_w, a_w, b_w = [windows(n) for n in ("tab_w", "y_w", "st_w", "a_w", "b_w")]
+        tab_rows = tab.rearrange("(p t) j -> p t j", t=PACK)
+        l1 = load_list("l1", n1)
+        nc.sync.dma_start(out=tab_w[0][:, lo], in_=tab_rows[:, 0, :])
+        w2w = load_words("w2w", w2_words, H)
+        l3 = load_list("l3", n3)
+        for t in range(1, PACK):
+            nc.sync.dma_start(out=tab_w[t][:, lo], in_=tab_rows[:, t, :])
+        w2s = load_scales("w2s", w2_scales, H)
+        gain = sb("gain", [P, PACK], F32)
+        nc.sync.dma_start(out=gain[:], in_=gn.rearrange("(p t) o -> p (t o)", t=PACK))
+        l2 = load_list("l2", n2)
+        l4 = load_list("l4", n4)
+        l5 = load_list("l5", n5)
+        l6 = load_list("l6", n6)
+        for t in tiles:
+            nc.vector.memset(tab_w[t][:, hi], 0.0)
+
+        xg = sb("xg", [P, S], U32)
+        xsg = sb("xsg", [P, S], U8)
+        nc.vector.tensor_copy(out=xsg[:], in_=xs[:].indirect(l_offs[:]))
+        w1sd = deal("w1sd", w1s, U8, 16)
+        nc.vector.tensor_copy(out=xg[:], in_=xw[:].indirect(l_offs[:]))
+        w1d = deal("w1d", w1w, U32, 4)
+        for t in tiles:
+            acc = product("y%d" % t, w1d, w1sd, [(xg, xsg, whole)], t)
+            nc.scalar.copy(out=y_w[t][:, lo], in_=acc[:])
+        w2d = deal("w2d", w2w, U32, 4)
+        w2sd = deal("w2sd", w2s, U8, 16)
+
+        for t in tiles:
+            nc.vector.tensor_tensor(y_w[t][:, hi], tab_w[t][:].indirect(l1[:]), y_w[t][:, lo], ALU.add)
+            nc.scalar.activation(st_w[t][:, hi], y_w[t][:].indirect(l3[:]), ACT.Sigmoid)
+
+        gst = sb("gst", [P, PACK, S], F32)
+        for t in tiles:
+            nc.vector.scalar_tensor_tensor(gst[:, t, :], y_w[t][:, lo], gain[:, t : t + 1], st_w[t][:, hi], ALU.mult, ALU.mult)
+            nc.scalar.activation(st_w[t][:, lo], gst[:, t, :], ACT.Copy, scale=-1.0)
+
+        z = sb("z", [P, PACK, S], F32)
+        for t in tiles:
+            nc.vector.tensor_copy(out=b_w[t][:, hi], in_=y_w[t][:].indirect(l2[:]))
+            nc.vector.tensor_tensor(a_w[t][:, hi], y_w[t][:, hi], b_w[t][:, hi], ALU.max)
+            nc.scalar.activation(z[:, t, :], a_w[t][:, hi], ACT.Copy, scale=gain[:, t : t + 1])
+        z_woven = sb("z_woven", [P, S, PACK], BF16)
+        weave(nc.scalar.copy, z_woven[:], z[:])
+        zq = [quantise("zq", z_woven, S) + (whole,)]
+
+        z2q = []
+        width = S // 2
+        for h in range(2):
+            span = slice(width * h, width * (h + 1))
+            z2 = sb("z2_%d" % h, [P, PACK, width], F32)
+            for t in tiles:
+                offsets = l4[:, width * h // 16 : width * (h + 1) // 16]
+                nc.vector.tensor_tensor(z2[:, t, :], st_w[t][:].indirect(offsets), gst[:, t, span], ALU.add)
+            z2_woven = sb("z2_woven%d" % h, [P, width, PACK], BF16)
+            weave(nc.scalar.copy, z2_woven[:], z2[:])
+            z2q.append(quantise("z2q%d" % h, z2_woven, width) + (span,))
+
+        a_plain = sb("a_plain", [P, PACK, S], F32)
+        for t in tiles:
+            acc = product("a%d" % t, w2d, w2sd, zq, t)
+            nc.scalar.copy(out=a_w[t][:, lo], in_=acc[:])
+            nc.scalar.copy(out=a_plain[:, t, :], in_=acc[:])
+        b_plain = sb("b_plain", [P, PACK, S], F32)
+        for t in tiles:
+            acc = product("b%d" % t, w2d, w2sd, z2q, t)
+            nc.scalar.copy(out=b_w[t][:, lo], in_=acc[:])
+            nc.scalar.copy(out=b_plain[:, t, :], in_=acc[:])
+
+        a_sum = sb("a_sum", [P, PACK, S], F32)
+        b_sum = sb("b_sum", [P, PACK, S], F32)
+        gate = sb("gate", [P, PACK, S], F32)
+        res = sb("res", [P, PACK, S], F32)
+        out_rows = out_0.rearrange("(p t) j -> p t j", t=PACK)
+        for t in tiles:
+            nc.vector.tensor_tensor(a_sum[:, t, :], a_w[t][:].indirect(l5[:]), a_plain[:, t, :], ALU.add)
+        for t in tiles:
+            nc.vector.tensor_tensor(b_sum[:, t, :], b_w[t][:].indirect(l6[:]), b_plain[:, t, :], ALU.add)
+            nc.scalar.activation(gate[:, t, :], b_sum[:, t, :], ACT.Sigmoid)
+        for t in tiles:
+            nc.vector.tensor_tensor(res[:, t, :], a_sum[:, t, :], gate[:, t, :], ALU.mult)
+            nc.sync.dma_start(out=out_rows[:, t, :], in_=res[:, t, :])
+        woven = sb("res_woven", [P, S, PACK], BF16)
+        cut = 160
+        weave(nc.scalar.copy, woven[:, :cut, :], res[:, :, :cut])
+        weave(nc.vector.tensor_copy, woven[:, cut:, :], res[:, :, cut:])
+        words, scales = quantise("res_q", woven, S)
+        nc.sync.dma_start(out=out_1[0].rearrange("p n t -> p (n t)").bitcast(I32), in_=words[:].bitcast(I32))
+        for q in range(4):
+            nc.scalar.dma_start(out=out_2[0, 4 * q : 4 * q + 4, :].bitcast(I32), in_=scales[32 * q : 32 * q + 4, :].bitcast(I32))

@@ -29,8 +29,8 @@ def tile_picked_tietriebkindhopg_none_po_kernel(
         keep = ctx.enter_context(tc.tile_pool(name="keep", bufs=1))
         psum = ctx.enter_context(tc.psum_pool(name="psum", bufs=1))
 
-        def sb(name, shape, dtype):
-            return keep.tile(shape, dtype, name=name, align_bytes=64)
+        def sb(name, shape, dtype, tag=None):
+            return keep.tile(shape, dtype, name=name, tag=tag or name, align_bytes=64)
 
         def load_list(name, src):
             tile = keep.tile([P, S // 16], U16, name=name)
@@ -42,33 +42,25 @@ def tile_picked_tietriebkindhopg_none_po_kernel(
             nc.sync.dma_start(out=tile[:].bitcast(I32), in_=src[0].rearrange("p n t -> p (n t)").bitcast(I32))
             return tile
 
-        def load_scales(name, src, width):
-            tile = sb(name, [P, width], U8)
-            nc.vector.memset(tile[:].bitcast(I32), 0)
-            for q in range(4):
-                nc.sync.dma_start(out=tile[32 * q : 32 * q + 4, :].bitcast(I32), in_=src[0, 4 * q : 4 * q + 4, :].bitcast(I32))
-            return tile
+        def load_scale_rows(tile, src, first, quadrants):
+            for q in quadrants:
+                rows = slice(32 * q + first, 32 * q + first + 4)
+                nc.sync.dma_start(out=tile[rows, :].bitcast(I32), in_=src[0, 4 * q : 4 * q + 4, :].bitcast(I32))
 
-        def load_scales_spread(tile, src, width, qs):
-            for q in qs:
-                rows = src[0, 4 * q : 4 * q + 4, :].bitcast(I32).unsqueeze(0).broadcast_to([8, 4, width // 4])
-                nc.sync.dma_start(out=tile[32 * q : 32 * q + 32, :].bitcast(I32), in_=rows)
-
-        def deal(name, tile, dtype, run):
-            dealt = sb(name, [P, H], dtype)
+        def deal(dealt, tile, run, ts):
             nc.vector.tensor_copy(
-                out=dealt[:].rearrange("p (t c i) -> p c t i", t=PACK, i=run),
-                in_=tile[:].rearrange("p (c i t) -> p c t i", t=PACK, i=run),
+                out=dealt[:].rearrange("p (t c i) -> p c t i", t=PACK, i=run)[:, :, ts, :],
+                in_=tile[:].rearrange("p (c i t) -> p c t i", t=PACK, i=run)[:, :, ts, :],
             )
-            return dealt
 
-        def product(name, words, scales, parts, t):
-            acc = psum.tile([P, S], F32, name=name, tag="bank%d" % (t + (4 if name[0] == "a" else 0)))
+        def product(name, bank, words, scales, t, parts):
+            acc = psum.tile([P, sum(span.stop - span.start for part in parts for span in part[2:])], F32, name=name, tag="bank%d" % bank)
             cols = slice(P * t, P * (t + 1))
+            first = parts[0][2].start
             for rhs_words, rhs_scales, span in parts:
                 nc.tensor.matmul_mx(
-                    out=acc[:, span], lhsT=words[:, cols].bitcast(FP8X4), lhsT_scale=scales[:, cols],
-                    rhs=rhs_words[:].bitcast(FP8X4), rhs_scale=rhs_scales[:], start=True, stop=True,
+                    out=acc[:, span.start - first : span.stop - first], lhsT=words[:, cols].bitcast(FP8X4), lhsT_scale=scales[:, cols],
+                    rhs=rhs_words.bitcast(FP8X4), rhs_scale=rhs_scales, start=True, stop=True,
                 )
             return acc
 
@@ -77,6 +69,9 @@ def tile_picked_tietriebkindhopg_none_po_kernel(
                 out=woven.rearrange("p (c i) t -> p c t i", i=4),
                 in_=planes.rearrange("p t (c i) -> p c t i", i=4),
             )
+
+        def negated(out, in_):
+            nc.scalar.activation(out, in_, ACT.Copy, scale=-1.0)
 
         def quantise(name, woven, width):
             words = sb(name + "_words", [P, width], U32)
@@ -88,15 +83,20 @@ def tile_picked_tietriebkindhopg_none_po_kernel(
             return [sb("%s%d" % (name, t), [P, 2 * S], F32) for t in tiles]
 
         lo, hi = slice(0, S), slice(S, 2 * S)
-        whole = slice(0, S)
+        halves = [slice(0, S // 2), slice(S // 2, S)]
 
         l_offs = load_list("l_offs", offs)
         xs = sb("xs", [P, T], U8)
-        load_scales_spread(xs, x_scales, T, range(4))
+        for q in range(4):
+            rows = x_scales[0, 4 * q : 4 * q + 4, :].bitcast(I32).unsqueeze(0).broadcast_to([8, 4, T // 4])
+            nc.sync.dma_start(out=xs[32 * q : 32 * q + 32, :].bitcast(I32), in_=rows)
+        ws = sb("ws", [P, H], U8)
+        nc.vector.memset(ws[:].bitcast(I32), 0)
+        load_scale_rows(ws, w1_scales, 0, range(2))
         xw = load_words("xw", x_words, T)
-        w1s = sb("w1s", [P, H], U8)
-        load_scales_spread(w1s, w1_scales, H, range(4))
+        load_scale_rows(ws, w1_scales, 0, range(2, 4))
         w1w = load_words("w1w", w1_words, H)
+        load_scale_rows(ws, w2_scales, 4, range(4))
         tab_w, y_w, st_w, a_w, b_w = [windows(n) for n in ("tab_w", "y_w", "st_w", "a_w", "b_w")]
         tab_rows = tab.rearrange("(p t) j -> p t j", t=PACK)
         l1 = load_list("l1", n1)
@@ -105,66 +105,78 @@ def tile_picked_tietriebkindhopg_none_po_kernel(
         l3 = load_list("l3", n3)
         for t in range(1, PACK):
             nc.sync.dma_start(out=tab_w[t][:, lo], in_=tab_rows[:, t, :])
-        w2s = load_scales("w2s", w2_scales, H)
         gain = sb("gain", [P, PACK], F32)
         nc.sync.dma_start(out=gain[:], in_=gn.rearrange("(p t) o -> p (t o)", t=PACK))
         l2 = load_list("l2", n2)
         l4 = load_list("l4", n4)
         l5 = load_list("l5", n5)
         l6 = load_list("l6", n6)
-        for t in tiles:
-            nc.vector.memset(tab_w[t][:, hi], 0.0)
 
-        xg = sb("xg", [P, S], U32)
         xsg = sb("xsg", [P, S], U8)
+        xg = sb("xg", [P, S], U32)
         nc.vector.tensor_copy(out=xsg[:], in_=xs[:].indirect(l_offs[:]))
-        w1sd = deal("w1sd", w1s, U8, 16)
         nc.vector.tensor_copy(out=xg[:], in_=xw[:].indirect(l_offs[:]))
-        w1d = deal("w1d", w1w, U32, 4)
+        wsd = sb("wsd", [P, H], U8)
+        w1d = sb("w1d", [P, H], U32)
+        w2d = sb("w2d", [P, H], U32)
+        for ts in (slice(0, 1), slice(1, PACK)):
+            deal(wsd, ws, 16, ts)
+            deal(w1d, w1w, 4, ts)
         for t in tiles:
-            acc = product("y%d" % t, w1d, w1sd, [(xg, xsg, whole)], t)
-            nc.scalar.copy(out=y_w[t][:, lo], in_=acc[:])
-        w2d = deal("w2d", w2w, U32, 4)
-        w2sd = deal("w2sd", w2s, U8, 16)
+            for h, span in enumerate(halves if t == 0 else [lo]):
+                acc = product("y%d_%d" % (t, h), t + 4 * h, w1d, wsd, t, [(xg[:, span], xsg[:, span], span)])
+                nc.scalar.copy(out=y_w[t][:, span], in_=acc[:])
+        deal(w2d, w2w, 4, slice(0, PACK))
+        w2sd = wsd[4:P, :]
 
+        sig = sb("sig", [P, PACK, S], F32)
         for t in tiles:
-            nc.vector.tensor_tensor(y_w[t][:, hi], tab_w[t][:].indirect(l1[:]), y_w[t][:, lo], ALU.add)
-            nc.scalar.activation(st_w[t][:, hi], y_w[t][:].indirect(l3[:]), ACT.Sigmoid)
+            for span in halves if t == 0 else [lo]:
+                offsets = l1[:, span.start // 16 : span.stop // 16]
+                nc.vector.tensor_tensor(y_w[t][:, S + span.start : S + span.stop], tab_w[t][:].indirect(offsets), y_w[t][:, span], ALU.add)
+            nc.scalar.activation(sig[:, t, :], y_w[t][:].indirect(l3[:]), ACT.Sigmoid)
 
+        looked = sb("looked", [P, PACK, S], F32)
+        for t in tiles:
+            nc.vector.tensor_copy(out=looked[:, t, :], in_=y_w[t][:].indirect(l2[:]))
+
+        st = sb("st", [P, PACK, S], F32, tag="tab_w3")
         gst = sb("gst", [P, PACK, S], F32)
         for t in tiles:
-            nc.vector.scalar_tensor_tensor(gst[:, t, :], y_w[t][:, lo], gain[:, t : t + 1], st_w[t][:, hi], ALU.mult, ALU.mult)
-            nc.scalar.activation(st_w[t][:, lo], gst[:, t, :], ACT.Copy, scale=-1.0)
+            nc.gpsimd.tensor_tensor(st[:, t, :], y_w[t][:, lo], sig[:, t, :], ALU.mult)
+            nc.scalar.activation(st_w[t][:, lo], st[:, t, :], ACT.Copy, scale=gain[:, t : t + 1])
+            nc.sync.dma_start(out=gst[:, t, :], in_=st_w[t][:, lo])
 
+        larger = sb("larger", [P, PACK, S], F32, tag="sig")
         z = sb("z", [P, PACK, S], F32)
         for t in tiles:
-            nc.vector.tensor_copy(out=b_w[t][:, hi], in_=y_w[t][:].indirect(l2[:]))
-            nc.vector.tensor_tensor(a_w[t][:, hi], y_w[t][:, hi], b_w[t][:, hi], ALU.max)
-            nc.scalar.activation(z[:, t, :], a_w[t][:, hi], ACT.Copy, scale=gain[:, t : t + 1])
+            nc.vector.tensor_tensor(larger[:, t, :], y_w[t][:, hi], looked[:, t, :], ALU.max)
+            nc.scalar.activation(z[:, t, :], larger[:, t, :], ACT.Copy, scale=gain[:, t : t + 1])
         z_woven = sb("z_woven", [P, S, PACK], BF16)
         weave(nc.scalar.copy, z_woven[:], z[:])
-        zq = [quantise("zq", z_woven, S) + (whole,)]
+        z_words, z_scales = quantise("zq", z_woven, S)
+        zq = [(z_words[:], z_scales[:], lo)]
 
         z2q = []
-        width = S // 2
-        for h in range(2):
-            span = slice(width * h, width * (h + 1))
-            z2 = sb("z2_%d" % h, [P, PACK, width], F32)
+        z2_both = sb("z2", [P, 2, PACK, S // 2], F32, tag="looked")
+        for h, span in enumerate(halves):
+            z2 = z2_both[:, h]
             for t in tiles:
-                offsets = l4[:, width * h // 16 : width * (h + 1) // 16]
-                nc.vector.tensor_tensor(z2[:, t, :], st_w[t][:].indirect(offsets), gst[:, t, span], ALU.add)
-            z2_woven = sb("z2_woven%d" % h, [P, width, PACK], BF16)
-            weave(nc.scalar.copy, z2_woven[:], z2[:])
-            z2q.append(quantise("z2q%d" % h, z2_woven, width) + (span,))
+                offsets = l4[:, span.start // 16 : span.stop // 16]
+                nc.vector.tensor_tensor(z2[:, t, :], st_w[t][:].indirect(offsets), gst[:, t, span], ALU.subtract)
+            z2_woven = sb("z2_woven%d" % h, [P, S // 2, PACK], BF16)
+            weave(negated, z2_woven[:], z2)
+            z2_words, z2_scales = quantise("z2q%d" % h, z2_woven, S // 2)
+            z2q.append((z2_words[:], z2_scales[:], span))
 
         a_plain = sb("a_plain", [P, PACK, S], F32)
         for t in tiles:
-            acc = product("a%d" % t, w2d, w2sd, zq, t)
+            acc = product("a%d" % t, 4 + t, w2d, w2sd, t, zq)
             nc.scalar.copy(out=a_w[t][:, lo], in_=acc[:])
             nc.scalar.copy(out=a_plain[:, t, :], in_=acc[:])
         b_plain = sb("b_plain", [P, PACK, S], F32)
         for t in tiles:
-            acc = product("b%d" % t, w2d, w2sd, z2q, t)
+            acc = product("b%d" % t, t, w2d, w2sd, t, z2q)
             nc.scalar.copy(out=b_w[t][:, lo], in_=acc[:])
             nc.scalar.copy(out=b_plain[:, t, :], in_=acc[:])
 

@@ -73,10 +73,13 @@ def tile_picked_tietriebkindhopg_none_po_kernel(
         def negated(out, in_):
             nc.scalar.activation(out, in_, ACT.Copy, scale=-1.0)
 
+        def negated_on_vector(out, in_):
+            nc.vector.tensor_scalar(out, in_, -1.0, None, ALU.mult)
+
         def quantise(name, woven, width):
             words = sb(name + "_words", [P, width], U32)
             scales = sb(name + "_scales", [P, width], U8)
-            nc.vector.quantize_mx(out=words[:].bitcast(FP8X4), scales=scales[:], in_=woven[:].rearrange("p n t -> p (n t)"))
+            nc.vector.quantize_mx(out=words[:].bitcast(FP8X4), scales=scales[:], in_=woven.rearrange("p n t -> p (n t)"))
             return words, scales
 
         def windows(name):
@@ -86,24 +89,25 @@ def tile_picked_tietriebkindhopg_none_po_kernel(
         halves = [slice(0, S // 2), slice(S // 2, S)]
 
         l_offs = load_list("l_offs", offs)
+        w1s = sb("w1s", [P, H], U8)
         xs = sb("xs", [P, T], U8)
-        for q in range(4):
-            rows = x_scales[0, 4 * q : 4 * q + 4, :].bitcast(I32).unsqueeze(0).broadcast_to([8, 4, T // 4])
-            nc.sync.dma_start(out=xs[32 * q : 32 * q + 32, :].bitcast(I32), in_=rows)
-        ws = sb("ws", [P, H], U8)
-        nc.vector.memset(ws[:].bitcast(I32), 0)
-        load_scale_rows(ws, w1_scales, 0, range(2))
-        xw = load_words("xw", x_words, T)
-        load_scale_rows(ws, w1_scales, 0, range(2, 4))
+        w2s = sb("w2s", [P, H], U8)
+        for plane in (w1s, xs, w2s):
+            nc.vector.memset(plane[:].bitcast(I32), 0)
         w1w = load_words("w1w", w1_words, H)
-        load_scale_rows(ws, w2_scales, 4, range(4))
+        load_scale_rows(w1s, w1_scales, 0, range(1))
+        load_scale_rows(xs, x_scales, 0, range(4))
+        xw = load_words("xw", x_words, T)
+        load_scale_rows(w1s, w1_scales, 0, range(1, 4))
         tab_w, y_w, st_w, a_w, b_w = [windows(n) for n in ("tab_w", "y_w", "st_w", "a_w", "b_w")]
         tab_rows = tab.rearrange("(p t) j -> p t j", t=PACK)
         l1 = load_list("l1", n1)
         nc.sync.dma_start(out=tab_w[0][:, lo], in_=tab_rows[:, 0, :])
-        w2w = load_words("w2w", w2_words, H)
         l3 = load_list("l3", n3)
-        for t in range(1, PACK):
+        nc.sync.dma_start(out=tab_w[1][:, lo], in_=tab_rows[:, 1, :])
+        w2w = load_words("w2w", w2_words, H)
+        load_scale_rows(w2s, w2_scales, 0, range(4))
+        for t in range(2, PACK):
             nc.sync.dma_start(out=tab_w[t][:, lo], in_=tab_rows[:, t, :])
         gain = sb("gain", [P, PACK], F32)
         nc.sync.dma_start(out=gain[:], in_=gn.rearrange("(p t) o -> p (t o)", t=PACK))
@@ -119,15 +123,17 @@ def tile_picked_tietriebkindhopg_none_po_kernel(
         wsd = sb("wsd", [P, H], U8)
         w1d = sb("w1d", [P, H], U32)
         w2d = sb("w2d", [P, H], U32)
+        deal(w1d, w1w, 4, slice(0, PACK))
         for ts in (slice(0, 1), slice(1, PACK)):
-            deal(wsd, ws, 16, ts)
-            deal(w1d, w1w, 4, ts)
+            deal(wsd, w1s, 16, ts)
         for t in tiles:
             for h, span in enumerate(halves if t == 0 else [lo]):
                 acc = product("y%d_%d" % (t, h), t + 4 * h, w1d, wsd, t, [(xg[:, span], xsg[:, span], span)])
                 nc.scalar.copy(out=y_w[t][:, span], in_=acc[:])
+        y_last = acc
         deal(w2d, w2w, 4, slice(0, PACK))
-        w2sd = wsd[4:P, :]
+        w2sd = sb("w2sd", [P, H], U8)
+        deal(w2sd, w2s, 16, slice(0, PACK))
 
         sig = sb("sig", [P, PACK, S], F32)
         for t in tiles:
@@ -143,7 +149,11 @@ def tile_picked_tietriebkindhopg_none_po_kernel(
         st = sb("st", [P, PACK, S], F32, tag="tab_w3")
         gst = sb("gst", [P, PACK, S], F32)
         for t in tiles:
-            nc.gpsimd.tensor_tensor(st[:, t, :], y_w[t][:, lo], sig[:, t, :], ALU.mult)
+            if t < PACK - 1:
+                nc.gpsimd.tensor_tensor(st[:, t, :], y_w[t][:, lo], sig[:, t, :], ALU.mult)
+            else:
+                nc.gpsimd.tensor_tensor(st[:, t, halves[0]], y_w[t][:, halves[0]], sig[:, t, halves[0]], ALU.mult)
+                nc.vector.tensor_tensor(st[:, t, halves[1]], y_last[:, halves[1]], sig[:, t, halves[1]], ALU.mult)
             nc.scalar.activation(st_w[t][:, lo], st[:, t, :], ACT.Copy, scale=gain[:, t : t + 1])
             nc.sync.dma_start(out=gst[:, t, :], in_=st_w[t][:, lo])
 
@@ -152,21 +162,21 @@ def tile_picked_tietriebkindhopg_none_po_kernel(
         for t in tiles:
             nc.vector.tensor_tensor(larger[:, t, :], y_w[t][:, hi], looked[:, t, :], ALU.max)
             nc.scalar.activation(z[:, t, :], larger[:, t, :], ACT.Copy, scale=gain[:, t : t + 1])
-        z_woven = sb("z_woven", [P, S, PACK], BF16)
-        weave(nc.scalar.copy, z_woven[:], z[:])
+        shared = sb("shared", [P, 5 * S], F32, tag="looked")
+        z_woven = shared[:, 3 * S :].bitcast(BF16).rearrange("p (n t) -> p n t", t=PACK)
+        weave(nc.scalar.copy, z_woven, z[:])
         z_words, z_scales = quantise("zq", z_woven, S)
         zq = [(z_words[:], z_scales[:], lo)]
 
         z2q = []
-        z2_both = sb("z2", [P, 2, PACK, S // 2], F32, tag="looked")
         for h, span in enumerate(halves):
-            z2 = z2_both[:, h]
+            z2 = shared[:, 2 * S * h : 2 * S * (h + 1)].rearrange("p (t n) -> p t n", t=PACK)
             for t in tiles:
                 offsets = l4[:, span.start // 16 : span.stop // 16]
                 nc.vector.tensor_tensor(z2[:, t, :], st_w[t][:].indirect(offsets), gst[:, t, span], ALU.subtract)
             z2_woven = sb("z2_woven%d" % h, [P, S // 2, PACK], BF16)
-            weave(negated, z2_woven[:], z2)
-            z2_words, z2_scales = quantise("z2q%d" % h, z2_woven, S // 2)
+            weave(negated_on_vector if h else negated, z2_woven[:], z2)
+            z2_words, z2_scales = quantise("z2q%d" % h, z2_woven[:], S // 2)
             z2q.append((z2_words[:], z2_scales[:], span))
 
         a_plain = sb("a_plain", [P, PACK, S], F32)
@@ -197,7 +207,7 @@ def tile_picked_tietriebkindhopg_none_po_kernel(
         cut = 160
         weave(nc.scalar.copy, woven[:, :cut, :], res[:, :, :cut])
         weave(nc.vector.tensor_copy, woven[:, cut:, :], res[:, :, cut:])
-        words, scales = quantise("res_q", woven, S)
+        words, scales = quantise("res_q", woven[:], S)
         nc.sync.dma_start(out=out_1[0].rearrange("p n t -> p (n t)").bitcast(I32), in_=words[:].bitcast(I32))
         for q in range(4):
             nc.scalar.dma_start(out=out_2[0, 4 * q : 4 * q + 4, :].bitcast(I32), in_=scales[32 * q : 32 * q + 4, :].bitcast(I32))

from contextlib import ExitStack

import concourse.mybir as mybir

F32 = mybir.dt.float32
BF16 = mybir.dt.bfloat16
I32 = mybir.dt.int32
U32 = mybir.dt.uint32
U16 = mybir.dt.uint16
U8 = mybir.dt.uint8
FP8X4 = mybir.dt.float8_e4m3fn_x4
ALU = mybir.AluOpType
ACT = mybir.ActivationFunctionType

P = 128
PACK = 4
T = 2048
S = 512
H = 512
FLOPS = 3 * 2 * 512 * 512 * 512


def tile_picked_tietriebkindhopg_none_po_kernel(
    tc, x_words, x_scales, w1_words, w1_scales, tab, gn, w2_words, w2_scales, offs, n1, n2, n3, n4, n5, n6, out_0, out_1, out_2
):
    nc = tc.nc
    tiles = range(PACK)
    with ExitStack() as ctx:
        keep = ctx.enter_context(tc.tile_pool(name="keep", bufs=1))
        psum = ctx.enter_context(tc.psum_pool(name="psum", bufs=1))

        def sb(name, shape, dtype, tag=None):
            return keep.tile(shape, dtype, name=name, tag=tag or name, align_bytes=64)

        def load_list(name, src):
            tile = keep.tile([P, S // 16], U16, name=name)
            nc.sync.dma_start(tile[:], src)
            return tile

        def load_words(name, src, width):
            tile = sb(name, [P, width], U32)
            nc.sync.dma_start(out=tile[:].bitcast(I32), in_=src[0].rearrange("p n t -> p (n t)").bitcast(I32))
            return tile

        def load_scale_rows(tile, src, first, quadrants):
            for q in quadrants:
                rows = slice(32 * q + first, 32 * q + first + 4)
                nc.sync.dma_start(out=tile[rows, :].bitcast(I32), in_=src[0, 4 * q : 4 * q + 4, :].bitcast(I32))

        def deal(dealt, tile, run, ts):
            nc.vector.tensor_copy(
                out=dealt[:].rearrange("p (t c i) -> p c t i", t=PACK, i=run)[:, :, ts, :],
                in_=tile[:].rearrange("p (c i t) -> p c t i", t=PACK, i=run)[:, :, ts, :],
            )

        def product(name, bank, words, scales, t, parts):
            acc = psum.tile([P, sum(span.stop - span.start for part in parts for span in part[2:])], F32, name=name, tag="bank%d" % bank)
            cols = slice(P * t, P * (t + 1))
            first = parts[0][2].start
            for rhs_words, rhs_scales, span in parts:
                nc.tensor.matmul_mx(
                    out=acc[:, span.start - first : span.stop - first], lhsT=words[:, cols].bitcast(FP8X4), lhsT_scale=scales[:, cols],
                    rhs=rhs_words.bitcast(FP8X4), rhs_scale=rhs_scales, start=True, stop=True,
                )
            return acc

        def weave(engine_copy, woven, planes):
            engine_copy(
                out=woven.rearrange("p (c i) t -> p c t i", i=4),
                in_=planes.rearrange("p t (c i) -> p c t i", i=4),
            )

        def negated(out, in_):
            nc.scalar.activation(out, in_, ACT.Copy, scale=-1.0)

        def negated_on_vector(out, in_):
            nc.vector.tensor_scalar(out, in_, -1.0, None, ALU.mult)

        def quantise(name, woven, width):
            words = sb(name + "_words", [P, width], U32)
            scales = sb(name + "_scales", [P, width], U8)
            nc.vector.quantize_mx(out=words[:].bitcast(FP8X4), scales=scales[:], in_=woven.rearrange("p n t -> p (n t)"))
            return words, scales

        def windows(name):
            return [sb("%s%d" % (name, t), [P, 2 * S], F32) for t in tiles]

        lo, hi = slice(0, S), slice(S, 2 * S)
        halves = [slice(0, S // 2), slice(S // 2, S)]

        l_offs = load_list("l_offs", offs)
        w1s = sb("w1s", [P, H], U8)
        xs = sb("xs", [P, T], U8)
        w2s = sb("w2s", [P, H], U8)
        for plane in (w1s, xs, w2s):
            nc.vector.memset(plane[:].bitcast(I32), 0)
        w1w = load_words("w1w", w1_words, H)
        load_scale_rows(w1s, w1_scales, 0, range(1))
        load_scale_rows(xs, x_scales, 0, range(4))
        xw = load_words("xw", x_words, T)
        load_scale_rows(w1s, w1_scales, 0, range(1, 4))
        tab_w, y_w, st_w, a_w, b_w = [windows(n) for n in ("tab_w", "y_w", "st_w", "a_w", "b_w")]
        tab_rows = tab.rearrange("(p t) j -> p t j", t=PACK)
        l1 = load_list("l1", n1)
        nc.sync.dma_start(out=tab_w[0][:, lo], in_=tab_rows[:, 0, :])
        l3 = load_list("l3", n3)
        nc.sync.dma_start(out=tab_w[1][:, lo], in_=tab_rows[:, 1, :])
        w2w = load_words("w2w", w2_words, H)
        load_scale_rows(w2s, w2_scales, 0, range(4))
        for t in range(2, PACK):
            nc.sync.dma_start(out=tab_w[t][:, lo], in_=tab_rows[:, t, :])
        gain = sb("gain", [P, PACK], F32)
        nc.sync.dma_start(out=gain[:], in_=gn.rearrange("(p t) o -> p (t o)", t=PACK))
        l2 = load_list("l2", n2)
        l4 = load_list("l4", n4)
        l5 = load_list("l5", n5)
        l6 = load_list("l6", n6)

        xsg = sb("xsg", [P, S], U8)
        xg = sb("xg", [P, S], U32)
        nc.vector.tensor_copy(out=xsg[:], in_=xs[:].indirect(l_offs[:]))
        nc.vector.tensor_copy(out=xg[:], in_=xw[:].indirect(l_offs[:]))
        wsd = sb("wsd", [P, H], U8)
        w1d = sb("w1d", [P, H], U32)
        w2d = sb("w2d", [P, H], U32)
        deal(w1d, w1w, 4, slice(0, PACK))
        for ts in (slice(0, 1), slice(1, PACK)):
            deal(wsd, w1s, 16, ts)
        for t in tiles:
            for h, span in enumerate(halves if t == 0 else [lo]):
                acc = product("y%d_%d" % (t, h), t + 4 * h, w1d, wsd, t, [(xg[:, span], xsg[:, span], span)])
                nc.scalar.copy(out=y_w[t][:, span], in_=acc[:])
        y_last = acc
        deal(w2d, w2w, 4, slice(0, PACK))
        w2sd = sb("w2sd", [P, H], U8)
        deal(w2sd, w2s, 16, slice(0, PACK))

        sig = sb("sig", [P, PACK, S], F32)
        for t in tiles:
            for span in halves if t == 0 else [lo]:
                offsets = l1[:, span.start // 16 : span.stop // 16]
                nc.vector.tensor_tensor(y_w[t][:, S + span.start : S + span.stop], tab_w[t][:].indirect(offsets), y_w[t][:, span], ALU.add)
            nc.scalar.activation(sig[:, t, :], y_w[t][:].indirect(l3[:]), ACT.Sigmoid)

        looked = sb("looked", [P, PACK, S], F32)
        for t in tiles:
            nc.vector.tensor_copy(out=looked[:, t, :], in_=y_w[t][:].indirect(l2[:]))

        st = sb("st", [P, PACK, S], F32, tag="tab_w3")
        gst = sb("gst", [P, PACK, S], F32)
        for t in tiles:
            if t < PACK - 1:
                nc.gpsimd.tensor_tensor(st[:, t, :], y_w[t][:, lo], sig[:, t, :], ALU.mult)
            else:
                nc.gpsimd.tensor_tensor(st[:, t, halves[0]], y_w[t][:, halves[0]], sig[:, t, halves[0]], ALU.mult)
                nc.vector.tensor_tensor(st[:, t, halves[1]], y_last[:, halves[1]], sig[:, t, halves[1]], ALU.mult)
            nc.scalar.activation(st_w[t][:, lo], st[:, t, :], ACT.Copy, scale=gain[:, t : t + 1])
            nc.sync.dma_start(out=gst[:, t, :], in_=st_w[t][:, lo])

        larger = sb("larger", [P, PACK, S], F32, tag="sig")
        z = sb("z", [P, PACK, S], F32)
        for t in tiles:
            nc.vector.tensor_tensor(larger[:, t, :], y_w[t][:, hi], looked[:, t, :], ALU.max)
            nc.scalar.activation(z[:, t, :], larger[:, t, :], ACT.Copy, scale=gain[:, t : t + 1])
        shared = sb("shared", [P, 5 * S], F32, tag="looked")
        z_woven = shared[:, 3 * S :].bitcast(BF16).rearrange("p (n t) -> p n t", t=PACK)
        weave(nc.scalar.copy, z_woven, z[:])
        z_words, z_scales = quantise("zq", z_woven, S)
        zq = [(z_words[:], z_scales[:], lo)]

        z2q = []
        for h, span in enumerate(halves):
            z2 = shared[:, 2 * S * h : 2 * S * (h + 1)].rearrange("p (t n) -> p t n", t=PACK)
            for t in tiles:
                offsets = l4[:, span.start // 16 : span.stop // 16]
                nc.vector.tensor_tensor(z2[:, t, :], st_w[t][:].indirect(offsets), gst[:, t, span], ALU.subtract)
            z2_woven = sb("z2_woven%d" % h, [P, S // 2, PACK], BF16)
            weave(negated_on_vector if h else negated, z2_woven[:], z2)
            z2_words, z2_scales = quantise("z2q%d" % h, z2_woven[:], S // 2)
            z2q.append((z2_words[:], z2_scales[:], span))

        a_plain = sb("a_plain", [P, PACK, S], F32)
        for t in tiles:
            acc = product("a%d" % t, 4 + t, w2d, w2sd, t, zq)
            nc.scalar.copy(out=a_w[t][:, lo], in_=acc[:])
            nc.scalar.copy(out=a_plain[:, t, :], in_=acc[:])
        b_plain = sb("b_plain", [P, PACK, S], F32)
        for t in tiles:
            acc = product("b%d" % t, t, w2d, w2sd, t, z2q)
            nc.scalar.copy(out=b_w[t][:, lo], in_=acc[:])
            nc.scalar.copy(out=b_plain[:, t, :], in_=acc[:])

        a_sum = sb("a_sum", [P, PACK, S], F32)
        b_sum = sb("b_sum", [P, PACK, S], F32)
        gate = sb("gate", [P, PACK, S], F32)
        res = sb("res", [P, PACK, S], F32)
        out_rows = out_0.rearrange("(p t) j -> p t j", t=PACK)
        for t in tiles:
            nc.vector.tensor_tensor(a_sum[:, t, :], a_w[t][:].indirect(l5[:]), a_plain[:, t, :], ALU.add)
        for t in tiles:
            nc.vector.tensor_tensor(b_sum[:, t, :], b_w[t][:].indirect(l6[:]), b_plain[:, t, :], ALU.add)
            nc.scalar.activation(gate[:, t, :], b_sum[:, t, :], ACT.Sigmoid)
        for t in tiles:
            nc.vector.tensor_tensor(res[:, t, :], a_sum[:, t, :], gate[:, t, :], ALU.mult)
            nc.sync.dma_start(out=out_rows[:, t, :], in_=res[:, t, :])
        woven = sb("res_woven", [P, S, PACK], BF16)
        cut = 160
        weave(nc.scalar.copy, woven[:, :cut, :], res[:, :, :cut])
        weave(nc.vector.tensor_copy, woven[:, cut:, :], res[:, :, cut:])
        words, scales = quantise("res_q", woven[:], S)
        nc.sync.dma_start(out=out_1[0].rearrange("p n t -> p (n t)").bitcast(I32), in_=words[:].bitcast(I32))
        for q in range(4):
            nc.scalar.dma_start(out=out_2[0, 4 * q : 4 * q + 4, :].bitcast(I32), in_=scales[32 * q : 32 * q + 4, :].bitcast(I32))
